import numpy as np
import ml_dtypes


def mxq(x, axis, fmt="e4m3"):
    dtype, down = {"e4m3": (ml_dtypes.float8_e4m3fn, 7), "e5m2": (ml_dtypes.float8_e5m2, 14)}[fmt]
    v = np.moveaxis(np.asarray(x, np.float32).astype(ml_dtypes.bfloat16).astype(np.float64), axis, -1)
    blocks = v.reshape(v.shape[:-1] + (-1, 32))
    amax = np.abs(blocks).max(-1, keepdims=True)
    byte = np.maximum(np.where(amax > 0, np.frexp(amax)[1] - 1 + 127, 0) - down, 1)
    scale = np.exp2(byte - 127.0)
    codes = (blocks / scale).astype(np.float32).astype(dtype).astype(np.float64)
    return np.moveaxis((codes * scale).reshape(v.shape), -1, axis)


WIDE = False


def mx_kscale(k):
    if not WIDE:
        return np.ones(k)
    levels = np.array([10, -10, 5, -5, 0])
    if k % 512:
        return np.exp2(np.random.permutation(np.resize(levels, k // 32))).repeat(32)
    a = np.empty((k // 512, 16))
    for p in range(k // 512):
        a[p, :8] = np.random.permutation(np.resize(levels, 8))
        for g in range(8):
            far = levels[np.abs(levels - a[p, g]) >= 10]
            a[p, g + 8] = far[np.random.randint(len(far))]
    return np.exp2(a.ravel()).repeat(32)


def f64(x):
    return np.asarray(x).astype(np.float64)


def striped(idx):
    return np.tile(np.asarray(idx).reshape(-1, 16).T, (8, 1)).astype(np.uint16)


def unstriped(offs):
    return offs[:16].T.reshape(-1).astype(np.int64)


E2M1 = np.array([0.0, 0.5, 1.0, 1.5, 2.0, 3.0, 4.0, 6.0, -0.0, -0.5, -1.0, -1.5, -2.0, -3.0, -4.0, -6.0])


def pack_weight(w, fmt):
    k, n = w.shape
    w = f64(np.asarray(w, np.float32).astype(ml_dtypes.bfloat16)).reshape(k // 32, 32, n)
    amax = np.abs(w).max(1)
    if fmt == "e4m3":
        byte = np.frexp(amax)[1] - 1 + 127 - 7
    else:
        mant, ex = np.frexp(amax / 6.0)
        byte = np.where(mant > 0.5, ex, ex - 1) + 127
    byte = np.clip(np.where(amax > 0, byte, 1), 1, 254)
    scaled = (w * np.exp2(127.0 - byte)[:, None, :]).reshape(k, n).astype(np.float32)
    by_word = np.ascontiguousarray(scaled.reshape(k // 512, 128, 4, n).transpose(0, 1, 3, 2))
    if fmt == "e4m3":
        words = by_word.astype(ml_dtypes.float8_e4m3fn).view(np.uint8)
    else:
        c = by_word.astype(ml_dtypes.float4_e2m1fn).view(np.uint8) & 0xF
        words = (c[..., 0::2] | (c[..., 1::2] << 4)).reshape(k // 512, 128, 2 * n)
    return np.ascontiguousarray(words), np.ascontiguousarray(byte.astype(np.uint8).reshape(k // 512, 16, n))


def unpack_weight(words, scales, fmt):
    g, _, n = scales.shape
    words = np.ascontiguousarray(words).reshape(g, 128, n, -1)
    if fmt == "e4m3":
        vals = words.view(ml_dtypes.float8_e4m3fn).astype(np.float64)
    else:
        nib = np.empty((g, 128, n, 4), np.uint8)
        nib[..., 0::2] = words & 0xF
        nib[..., 1::2] = words >> 4
        vals = E2M1[nib]
    vals = vals * np.repeat(np.exp2(scales.astype(np.float64) - 127.0), 8, axis=1)[..., None]
    return vals.transpose(0, 1, 3, 2).reshape(g * 512, n)


K, R, F, T, J, G = 512, 128, 512, 2048, 512, 32


def setup_inputs():
    n = np.random.standard_normal
    idx = np.random.permutation(T)[:J]
    fk = mx_kscale(K)
    tabp = pack_weight(n((K, T)) / fk[:, None], "e4m3")
    dtabp = pack_weight(n((K, T)) / fk[:, None], "e4m3")
    return {
        "tab_words": tabp[0],
        "tab_scales": tabp[1],
        "dtab_words": dtabp[0],
        "dtab_scales": dtabp[1],
        "w1": (n((K, R)) * 1 / np.sqrt(K) * fk[:, None]).astype(np.float32),
        "gain": (np.random.uniform(0.5, 1.5, (R, 1))).astype(np.float32),
        "bias": (np.random.uniform(-0.5, 0.5, (R, 1))).astype(np.float32),
        "og": (np.random.uniform(0.5, 2.0, (R, 1))).astype(np.float32),
        "base": (0.3 * n((R, J))).astype(np.float32),
        "offs": striped(idx),
    }


def reference(tab_words, tab_scales, dtab_words, dtab_scales, w1, gain, bias, og, base, offs):
    idx = unstriped(offs)
    tabu = unpack_weight(tab_words, tab_scales, "e4m3")
    dtabu = unpack_weight(dtab_words, dtab_scales, "e4m3")
    w1q = mxq(f64(w1), 0, "e4m3")
    tabidxg = tabu[:, idx]
    a = w1q.T @ tabidxg
    dtabidxg = dtabu[:, idx]
    ta = w1q.T @ dtabidxg
    m1 = a.reshape(R, G, J // G).mean(axis=2)
    mr = np.repeat(m1, J // G, axis=1)
    ce = a - mr
    v1 = np.sqrt(np.square(ce).reshape(R, G, J // G).mean(axis=2) + 0.05)
    vr = np.repeat(v1, J // G, axis=1)
    s = ce / vr * f64(gain) + f64(bias)
    u1 = np.tanh(s)
    tm1 = ta.reshape(R, G, J // G).mean(axis=2)
    tmr = np.repeat(tm1, J // G, axis=1)
    tce = ta - tmr
    tv1 = (tce * ce * 2.0).reshape(R, G, J // G).mean(axis=2) * 0.5 / v1
    tvr = np.repeat(tv1, J // G, axis=1)
    ts = (tce - tvr * ce / vr) / vr * f64(gain)
    tu1 = ts * (1.0 - np.square(u1))
    y = tu1 * f64(og) + f64(base)
    return y

@@ -1,0 +1,180 @@
+from contextlib import ExitStack
+
+import concourse.mybir as mybir
+
+K, R, T, J, G = 512, 128, 2048, 512, 32
+GROUP = J // G
+EPS = 0.05
+FLOPS = 2 * 2 * K * R * J
+
+F32 = mybir.dt.float32
+BF16 = mybir.dt.bfloat16
+I32 = mybir.dt.int32
+U32 = mybir.dt.uint32
+U16 = mybir.dt.uint16
+U8 = mybir.dt.uint8
+FP8X4 = mybir.dt.float8_e4m3fn_x4
+ALU = mybir.AluOpType
+ACT = mybir.ActivationFunctionType
+AXIS_X = mybir.AxisListType.X
+
+P = 128
+PACK = 4
+HALVES = 2
+HJ = J // HALVES
+HG = G // HALVES
+
+
+def tile_attend_tcgroupscale_kernel(
+    tc, tab_words, tab_scales, dtab_words, dtab_scales, w1, gain, bias, og, base, offs, out
+):
+    nc = tc.nc
+
+    def grouped(ap):
+        return ap.rearrange("p (g i) -> p g i", i=GROUP)
+
+    def spread(ap):
+        return ap.unsqueeze(2).to_broadcast([P, HG, GROUP])
+
+    with ExitStack() as ctx:
+        sb = ctx.enter_context(tc.tile_pool(name="sb", bufs=1))
+        ps = ctx.enter_context(tc.psum_pool(name="ps", bufs=1))
+
+        offsets = sb.tile([P, J // 16], U16, name="offsets")
+        nc.sync.dma_start(offsets[:], offs)
+
+        tab_plane = sb.tile([P, T], U8, name="tab_plane", tag="late_window", align_bytes=64)
+        dtab_plane = sb.tile([P, T], U8, name="dtab_plane", align_bytes=64)
+        nc.vector.memset(tab_plane[:].bitcast(I32), 0)
+        nc.vector.memset(dtab_plane[:].bitcast(I32), 0)
+
+        warm_in = sb.tile([P, 1], F32, name="warm_in")
+        warm_out = sb.tile([P, 1], F32, name="warm_out")
+        nc.gpsimd.memset(warm_in[:], 1.0)
+
+        w_raw = sb.tile([P, PACK, R], F32, name="w_raw", tag="rows")
+        nc.sync.dma_start(out=w_raw[:], in_=w1.rearrange("(p t) r -> p t r", t=PACK))
+
+        for q in range(4):
+            nc.scalar.dma_start(
+                out=tab_plane[32 * q : 32 * q + 4, :].bitcast(I32),
+                in_=tab_scales[0, 4 * q : 4 * q + 4, :].bitcast(I32),
+            )
+        tab_win = sb.tile([P, T], U32, name="tab_win")
+        nc.sync.dma_start(
+            out=tab_win[:].bitcast(I32), in_=tab_words[0].rearrange("p n t -> p (n t)").bitcast(I32)
+        )
+        for q in range(4):
+            nc.scalar.dma_start(
+                out=dtab_plane[32 * q : 32 * q + 4, :].bitcast(I32),
+                in_=dtab_scales[0, 4 * q : 4 * q + 4, :].bitcast(I32),
+            )
+        gain_c = sb.tile([P, 1], F32, name="gain_c")
+        bias_c = sb.tile([P, 1], F32, name="bias_c")
+        og_c = sb.tile([P, 1], F32, name="og_c")
+        nc.gpsimd.dma_start(out=gain_c[:], in_=gain)
+        nc.gpsimd.dma_start(out=bias_c[:], in_=bias)
+        nc.gpsimd.dma_start(out=og_c[:], in_=og)
+
+        nc.scalar.activation(warm_out[:], warm_in[:], ACT.Abs_reciprocal_sqrt)
+
+        w_bf = sb.tile([P, R, PACK], BF16, name="w_bf", align_bytes=64)
+        nc.vector.tensor_copy(w_bf[:], w_raw[:].rearrange("p t r -> p r t"))
+        w_codes = sb.tile([P, R], U32, name="w_codes", align_bytes=64)
+        w_scales = sb.tile([P, R], U8, name="w_scales", align_bytes=64)
+        nc.vector.quantize_mx(
+            out=w_codes[:].bitcast(FP8X4), scales=w_scales[:], in_=w_bf[:].rearrange("p r t -> p (r t)")
+        )
+
+        tab_sc = sb.tile([P, J], U8, name="tab_sc", align_bytes=64)
+        nc.vector.tensor_copy(tab_sc[:], tab_plane[:].indirect(offsets[:]))
+
+        dtab_win = sb.tile([P, T], U32, name="dtab_win", tag="late_window", align_bytes=64)
+        nc.sync.dma_start(
+            out=dtab_win[:].bitcast(I32), in_=dtab_words[0].rearrange("p n t -> p (n t)").bitcast(I32)
+        )
+
+        base_sb = sb.tile([P, J], F32, name="base_sb", tag="rows")
+        nc.sync.dma_start(out=base_sb[:], in_=base)
+
+        def product(window, scales, h, name):
+            cols = slice(h * HJ, (h + 1) * HJ)
+            codes = sb.tile([P, HJ], U32, name=name + "_codes%d" % h, align_bytes=64)
+            nc.vector.tensor_copy(codes[:], window[:].indirect(offsets[:, h * HG : (h + 1) * HG]))
+            acc = ps.tile([P, HJ], F32, name=name + "_acc%d" % h)
+            nc.tensor.matmul_mx(
+                out=acc[:],
+                lhsT=w_codes[:].bitcast(FP8X4),
+                lhsT_scale=w_scales[:],
+                rhs=codes[:].bitcast(FP8X4),
+                rhs_scale=scales[:, cols],
+                start=True,
+                stop=True,
+            )
+            return acc
+
+        def wide(name):
+            return [sb.tile([P, HJ], F32, name=name + "%d" % h) for h in range(HALVES)]
+
+        def narrow(name):
+            return [sb.tile([P, HG], F32, name=name + "%d" % h) for h in range(HALVES)]
+
+        halves = range(HALVES)
+        a = [product(tab_win, tab_sc, h, "a") for h in halves]
+
+        a_sum, ce, sq = narrow("a_sum"), wide("ce"), wide("sq")
+        var_sum = sb.tile([P, G], F32, name="var_sum")
+        for h in halves:
+            nc.vector.tensor_reduce(a_sum[h][:], grouped(a[h][:]), AXIS_X, ALU.add)
+            nc.vector.scalar_tensor_tensor(
+                grouped(ce[h][:]), spread(a_sum[h][:]), -1.0 / GROUP, grouped(a[h][:]), ALU.mult, ALU.add
+            )
+            nc.scalar.activation(sq[h][:], ce[h][:], ACT.Square)
+        for h in halves:
+            nc.vector.tensor_reduce(var_sum[:, h * HG : (h + 1) * HG], grouped(sq[h][:]), AXIS_X, ALU.add)
+        rstd = sb.tile([P, G], F32, name="rstd")
+        nc.scalar.activation(rstd[:], var_sum[:], ACT.Abs_reciprocal_sqrt, bias=EPS, scale=1.0 / GROUP)
+
+        dtab_sc = sb.tile([P, J], U8, name="dtab_sc", align_bytes=64)
+        nc.vector.tensor_copy(dtab_sc[:], dtab_plane[:].indirect(offsets[:]))
+        gains = sb.tile([P, 1], F32, name="gains")
+        nc.vector.tensor_tensor(gains[:], gain_c[:], og_c[:], ALU.mult)
+
+        n, u, u2 = wide("n"), wide("u"), wide("u2")
+        for h in halves:
+            nc.vector.tensor_tensor(
+                grouped(n[h][:]), grouped(ce[h][:]), spread(rstd[:, h * HG : (h + 1) * HG]), ALU.mult
+            )
+        for h in halves:
+            nc.scalar.activation(u[h][:], n[h][:], ACT.Tanh, bias=bias_c[:], scale=gain_c[:])
+            nc.scalar.activation(u2[h][:], u[h][:], ACT.Square)
+
+        ta = [product(dtab_win, dtab_sc, h, "ta") for h in halves]
+        t_sum, c = narrow("t_sum"), narrow("c")
+        tce, prod, along, x, wgt, t, y = (
+            wide("tce"), wide("prod"), wide("along"), wide("x"), wide("wgt"), wide("t"), wide("y")
+        )
+        for h in halves:
+            nc.vector.tensor_reduce(t_sum[h][:], grouped(ta[h][:]), AXIS_X, ALU.add)
+        for h in halves:
+            nc.vector.scalar_tensor_tensor(prod[h][:], ta[h][:], 1.0 / GROUP, n[h][:], ALU.mult, ALU.mult)
+        for h in halves:
+            nc.vector.tensor_reduce(c[h][:], grouped(prod[h][:]), AXIS_X, ALU.add)
+        for h in halves:
+            nc.vector.scalar_tensor_tensor(
+                grouped(tce[h][:]), spread(t_sum[h][:]), -1.0 / GROUP, grouped(ta[h][:]), ALU.mult, ALU.add
+            )
+        for h in halves:
+            nc.vector.tensor_tensor(grouped(along[h][:]), grouped(n[h][:]), spread(c[h][:]), ALU.mult)
+        for h in halves:
+            nc.vector.scalar_tensor_tensor(
+                grouped(wgt[h][:]), grouped(u2[h][:]), -1.0, spread(rstd[:, h * HG : (h + 1) * HG]), ALU.add, ALU.mult
+            )
+        for h in halves:
+            nc.vector.tensor_tensor(x[h][:], along[h][:], tce[h][:], ALU.subtract)
+        for h in halves:
+            nc.vector.scalar_tensor_tensor(t[h][:], x[h][:], gains[:], wgt[h][:], ALU.mult, ALU.mult)
+        for h in halves:
+            cols = slice(h * HJ, (h + 1) * HJ)
+            nc.vector.tensor_tensor(y[h][:], t[h][:], base_sb[:, cols], ALU.add)
+            nc.sync.dma_start(out=out[:, cols], in_=y[h][:])

@@ -43,7 +43,7 @@ def tile_attend_tcgroupscale_kernel(
         offsets = sb.tile([P, J // 16], U16, name="offsets")
         nc.sync.dma_start(offsets[:], offs)
 
-        tab_plane = sb.tile([P, T], U8, name="tab_plane", tag="late_window", align_bytes=64)
+        tab_plane = sb.tile([P, T], U8, name="tab_plane", align_bytes=64)
         dtab_plane = sb.tile([P, T], U8, name="dtab_plane", align_bytes=64)
         nc.vector.memset(tab_plane[:].bitcast(I32), 0)
         nc.vector.memset(dtab_plane[:].bitcast(I32), 0)
@@ -52,11 +52,11 @@ def tile_attend_tcgroupscale_kernel(
         warm_out = sb.tile([P, 1], F32, name="warm_out")
         nc.gpsimd.memset(warm_in[:], 1.0)
 
-        w_raw = sb.tile([P, PACK, R], F32, name="w_raw", tag="rows")
+        w_raw = sb.tile([P, PACK, R], F32, name="w_raw")
         nc.sync.dma_start(out=w_raw[:], in_=w1.rearrange("(p t) r -> p t r", t=PACK))
 
         for q in range(4):
-            nc.scalar.dma_start(
+            nc.sync.dma_start(
                 out=tab_plane[32 * q : 32 * q + 4, :].bitcast(I32),
                 in_=tab_scales[0, 4 * q : 4 * q + 4, :].bitcast(I32),
             )
@@ -65,16 +65,22 @@ def tile_attend_tcgroupscale_kernel(
             out=tab_win[:].bitcast(I32), in_=tab_words[0].rearrange("p n t -> p (n t)").bitcast(I32)
         )
         for q in range(4):
-            nc.scalar.dma_start(
+            nc.sync.dma_start(
                 out=dtab_plane[32 * q : 32 * q + 4, :].bitcast(I32),
                 in_=dtab_scales[0, 4 * q : 4 * q + 4, :].bitcast(I32),
             )
+        dtab_win = sb.tile([P, T], U32, name="dtab_win", tag="dtab_then_n")
+        nc.sync.dma_start(
+            out=dtab_win[:].bitcast(I32), in_=dtab_words[0].rearrange("p n t -> p (n t)").bitcast(I32)
+        )
         gain_c = sb.tile([P, 1], F32, name="gain_c")
         bias_c = sb.tile([P, 1], F32, name="bias_c")
         og_c = sb.tile([P, 1], F32, name="og_c")
-        nc.gpsimd.dma_start(out=gain_c[:], in_=gain)
-        nc.gpsimd.dma_start(out=bias_c[:], in_=bias)
-        nc.gpsimd.dma_start(out=og_c[:], in_=og)
+        nc.sync.dma_start(out=gain_c[:], in_=gain)
+        nc.sync.dma_start(out=bias_c[:], in_=bias)
+        nc.sync.dma_start(out=og_c[:], in_=og)
+        base_sb = sb.tile([P, J], F32, name="base_sb")
+        nc.sync.dma_start(out=base_sb[:], in_=base)
 
         nc.scalar.activation(warm_out[:], warm_in[:], ACT.Abs_reciprocal_sqrt)
 
@@ -88,14 +94,6 @@ def tile_attend_tcgroupscale_kernel(
 
         tab_sc = sb.tile([P, J], U8, name="tab_sc", align_bytes=64)
         nc.vector.tensor_copy(tab_sc[:], tab_plane[:].indirect(offsets[:]))
-
-        dtab_win = sb.tile([P, T], U32, name="dtab_win", tag="late_window", align_bytes=64)
-        nc.sync.dma_start(
-            out=dtab_win[:].bitcast(I32), in_=dtab_words[0].rearrange("p n t -> p (n t)").bitcast(I32)
-        )
-
-        base_sb = sb.tile([P, J], F32, name="base_sb", tag="rows")
-        nc.sync.dma_start(out=base_sb[:], in_=base)
 
         def product(window, scales, h, name):
             cols = slice(h * HJ, (h + 1) * HJ)
@@ -122,12 +120,14 @@ def tile_attend_tcgroupscale_kernel(
         halves = range(HALVES)
         a = [product(tab_win, tab_sc, h, "a") for h in halves]
 
-        a_sum, ce, sq = narrow("a_sum"), wide("ce"), wide("sq")
+        ce, sq = wide("ce"), wide("sq")
+        a_sum = sb.tile([P, G], F32, name="a_sum", tag="sum_then_scales", align_bytes=64)
         var_sum = sb.tile([P, G], F32, name="var_sum")
         for h in halves:
-            nc.vector.tensor_reduce(a_sum[h][:], grouped(a[h][:]), AXIS_X, ALU.add)
+            nc.vector.tensor_reduce(a_sum[:, h * HG : (h + 1) * HG], grouped(a[h][:]), AXIS_X, ALU.add)
+        for h in halves:
             nc.vector.scalar_tensor_tensor(
-                grouped(ce[h][:]), spread(a_sum[h][:]), -1.0 / GROUP, grouped(a[h][:]), ALU.mult, ALU.add
+                grouped(ce[h][:]), spread(a_sum[:, h * HG : (h + 1) * HG]), -1.0 / GROUP, grouped(a[h][:]), ALU.mult, ALU.add
             )
             nc.scalar.activation(sq[h][:], ce[h][:], ACT.Square)
         for h in halves:
@@ -135,21 +135,23 @@ def tile_attend_tcgroupscale_kernel(
         rstd = sb.tile([P, G], F32, name="rstd")
         nc.scalar.activation(rstd[:], var_sum[:], ACT.Abs_reciprocal_sqrt, bias=EPS, scale=1.0 / GROUP)
 
-        dtab_sc = sb.tile([P, J], U8, name="dtab_sc", align_bytes=64)
+        dtab_sc = sb.tile([P, J], U8, name="dtab_sc", tag="sum_then_scales", align_bytes=64)
         nc.vector.tensor_copy(dtab_sc[:], dtab_plane[:].indirect(offsets[:]))
         gains = sb.tile([P, 1], F32, name="gains")
         nc.vector.tensor_tensor(gains[:], gain_c[:], og_c[:], ALU.mult)
 
-        n, u, u2 = wide("n"), wide("u"), wide("u2")
+        ta = [product(dtab_win, dtab_sc, h, "ta") for h in halves]
+        u, u2 = wide("u"), wide("u2")
+        n_all = sb.tile([P, J], F32, name="n_all", tag="dtab_then_n")
+        n = [n_all[:, h * HJ : (h + 1) * HJ] for h in halves]
         for h in halves:
             nc.vector.tensor_tensor(
-                grouped(n[h][:]), grouped(ce[h][:]), spread(rstd[:, h * HG : (h + 1) * HG]), ALU.mult
+                grouped(n[h]), grouped(ce[h][:]), spread(rstd[:, h * HG : (h + 1) * HG]), ALU.mult
             )
         for h in halves:
-            nc.scalar.activation(u[h][:], n[h][:], ACT.Tanh, bias=bias_c[:], scale=gain_c[:])
+            nc.scalar.activation(u[h][:], n[h], ACT.Tanh, bias=bias_c[:], scale=gain_c[:])
             nc.scalar.activation(u2[h][:], u[h][:], ACT.Square)
 
-        ta = [product(dtab_win, dtab_sc, h, "ta") for h in halves]
         t_sum, c = narrow("t_sum"), narrow("c")
         tce, prod, along, x, wgt, t, y = (
             wide("tce"), wide("prod"), wide("along"), wide("x"), wide("wgt"), wide("t"), wide("y")
@@ -157,7 +159,7 @@ def tile_attend_tcgroupscale_kernel(
         for h in halves:
             nc.vector.tensor_reduce(t_sum[h][:], grouped(ta[h][:]), AXIS_X, ALU.add)
         for h in halves:
-            nc.vector.scalar_tensor_tensor(prod[h][:], ta[h][:], 1.0 / GROUP, n[h][:], ALU.mult, ALU.mult)
+            nc.vector.scalar_tensor_tensor(prod[h][:], ta[h][:], 1.0 / GROUP, n[h], ALU.mult, ALU.mult)
         for h in halves:
             nc.vector.tensor_reduce(c[h][:], grouped(prod[h][:]), AXIS_X, ALU.add)
         for h in halves:
@@ -165,7 +167,7 @@ def tile_attend_tcgroupscale_kernel(
                 grouped(tce[h][:]), spread(t_sum[h][:]), -1.0 / GROUP, grouped(ta[h][:]), ALU.mult, ALU.add
             )
         for h in halves:
-            nc.vector.tensor_tensor(grouped(along[h][:]), grouped(n[h][:]), spread(c[h][:]), ALU.mult)
+            nc.vector.tensor_tensor(grouped(along[h][:]), grouped(n[h]), spread(c[h][:]), ALU.mult)
         for h in halves:
             nc.vector.scalar_tensor_tensor(
                 grouped(wgt[h][:]), grouped(u2[h][:]), -1.0, spread(rstd[:, h * HG : (h + 1) * HG]), ALU.add, ALU.mult

@@ -44,7 +44,7 @@ def tile_attend_tcgroupscale_kernel(
         nc.sync.dma_start(offsets[:], offs)
 
         tab_plane = sb.tile([P, T], U8, name="tab_plane", align_bytes=64)
-        dtab_plane = sb.tile([P, T], U8, name="dtab_plane", align_bytes=64)
+        dtab_plane = sb.tile([P, T], U8, name="dtab_plane", tag="plane_then_sum", align_bytes=64)
         nc.vector.memset(tab_plane[:].bitcast(I32), 0)
         nc.vector.memset(dtab_plane[:].bitcast(I32), 0)
 
@@ -69,7 +69,7 @@ def tile_attend_tcgroupscale_kernel(
                 out=dtab_plane[32 * q : 32 * q + 4, :].bitcast(I32),
                 in_=dtab_scales[0, 4 * q : 4 * q + 4, :].bitcast(I32),
             )
-        dtab_win = sb.tile([P, T], U32, name="dtab_win", tag="dtab_then_n")
+        dtab_win = sb.tile([P, T], U32, name="dtab_win", tag="window_then_var")
         nc.sync.dma_start(
             out=dtab_win[:].bitcast(I32), in_=dtab_words[0].rearrange("p n t -> p (n t)").bitcast(I32)
         )
@@ -81,6 +81,9 @@ def tile_attend_tcgroupscale_kernel(
         nc.sync.dma_start(out=og_c[:], in_=og)
         base_sb = sb.tile([P, J], F32, name="base_sb")
         nc.sync.dma_start(out=base_sb[:], in_=base)
+
+        gains = sb.tile([P, 1], F32, name="gains")
+        nc.gpsimd.tensor_tensor(gains[:], gain_c[:], og_c[:], ALU.mult)
 
         nc.scalar.activation(warm_out[:], warm_in[:], ACT.Abs_reciprocal_sqrt)
 
@@ -120,9 +123,11 @@ def tile_attend_tcgroupscale_kernel(
         halves = range(HALVES)
         a = [product(tab_win, tab_sc, h, "a") for h in halves]
 
+        dtab_sc = sb.tile([P, J], U8, name="dtab_sc", align_bytes=64)
+        nc.vector.tensor_copy(dtab_sc[:], dtab_plane[:].indirect(offsets[:]))
+
         ce, sq = wide("ce"), wide("sq")
-        a_sum = sb.tile([P, G], F32, name="a_sum", tag="sum_then_scales", align_bytes=64)
-        var_sum = sb.tile([P, G], F32, name="var_sum")
+        a_sum = sb.tile([P, G], F32, name="a_sum", tag="plane_then_sum", align_bytes=64)
         for h in halves:
             nc.vector.tensor_reduce(a_sum[:, h * HG : (h + 1) * HG], grouped(a[h][:]), AXIS_X, ALU.add)
         for h in halves:
@@ -130,52 +135,78 @@ def tile_attend_tcgroupscale_kernel(
                 grouped(ce[h][:]), spread(a_sum[:, h * HG : (h + 1) * HG]), -1.0 / GROUP, grouped(a[h][:]), ALU.mult, ALU.add
             )
             nc.scalar.activation(sq[h][:], ce[h][:], ACT.Square)
+        ta = [product(dtab_win, dtab_sc, h, "ta") for h in halves]
+        var_sum = sb.tile([P, G], F32, name="var_sum", tag="window_then_var")
         for h in halves:
             nc.vector.tensor_reduce(var_sum[:, h * HG : (h + 1) * HG], grouped(sq[h][:]), AXIS_X, ALU.add)
         rstd = sb.tile([P, G], F32, name="rstd")
         nc.scalar.activation(rstd[:], var_sum[:], ACT.Abs_reciprocal_sqrt, bias=EPS, scale=1.0 / GROUP)
+        rvar = sb.tile([P, G], F32, name="rvar")
+        nc.gpsimd.tensor_tensor(rvar[:], rstd[:], rstd[:], ALU.mult)
 
-        dtab_sc = sb.tile([P, J], U8, name="dtab_sc", tag="sum_then_scales", align_bytes=64)
-        nc.vector.tensor_copy(dtab_sc[:], dtab_plane[:].indirect(offsets[:]))
-        gains = sb.tile([P, 1], F32, name="gains")
-        nc.vector.tensor_tensor(gains[:], gain_c[:], og_c[:], ALU.mult)
 
-        ta = [product(dtab_win, dtab_sc, h, "ta") for h in halves]
         u, u2 = wide("u"), wide("u2")
-        n_all = sb.tile([P, J], F32, name="n_all", tag="dtab_then_n")
+        n_all = sb.tile([P, J], F32, name="n_all")
         n = [n_all[:, h * HJ : (h + 1) * HJ] for h in halves]
         for h in halves:
-            nc.vector.tensor_tensor(
+            nc.gpsimd.tensor_tensor(
                 grouped(n[h]), grouped(ce[h][:]), spread(rstd[:, h * HG : (h + 1) * HG]), ALU.mult
             )
         for h in halves:
             nc.scalar.activation(u[h][:], n[h], ACT.Tanh, bias=bias_c[:], scale=gain_c[:])
             nc.scalar.activation(u2[h][:], u[h][:], ACT.Square)
 
-        t_sum, c = narrow("t_sum"), narrow("c")
+        t_sum, cov, c = narrow("t_sum"), narrow("cov"), narrow("c")
         tce, prod, along, x, wgt, t, y = (
             wide("tce"), wide("prod"), wide("along"), wide("x"), wide("wgt"), wide("t"), wide("y")
         )
-        for h in halves:
+
+        def sum_ta(h):
             nc.vector.tensor_reduce(t_sum[h][:], grouped(ta[h][:]), AXIS_X, ALU.add)
-        for h in halves:
-            nc.vector.scalar_tensor_tensor(prod[h][:], ta[h][:], 1.0 / GROUP, n[h], ALU.mult, ALU.mult)
-        for h in halves:
-            nc.vector.tensor_reduce(c[h][:], grouped(prod[h][:]), AXIS_X, ALU.add)
-        for h in halves:
+
+        def centre_ta(h):
             nc.vector.scalar_tensor_tensor(
                 grouped(tce[h][:]), spread(t_sum[h][:]), -1.0 / GROUP, grouped(ta[h][:]), ALU.mult, ALU.add
             )
-        for h in halves:
-            nc.vector.tensor_tensor(grouped(along[h][:]), grouped(n[h]), spread(c[h][:]), ALU.mult)
-        for h in halves:
-            nc.vector.scalar_tensor_tensor(
-                grouped(wgt[h][:]), grouped(u2[h][:]), -1.0, spread(rstd[:, h * HG : (h + 1) * HG]), ALU.add, ALU.mult
-            )
-        for h in halves:
+
+        def multiply(h):
+            nc.vector.scalar_tensor_tensor(prod[h][:], ta[h][:], 1.0 / GROUP, ce[h][:], ALU.mult, ALU.mult)
+
+        def project(h):
+            nc.vector.tensor_reduce(cov[h][:], grouped(prod[h][:]), AXIS_X, ALU.add)
+
+        def slope(h):
+            nc.vector.tensor_tensor(c[h][:], cov[h][:], rvar[:, h * HG : (h + 1) * HG], ALU.mult)
+
+        def along_n(h, engine):
+            engine.tensor_tensor(grouped(along[h][:]), grouped(ce[h][:]), spread(c[h][:]), ALU.mult)
+
+        def remove_along(h):
             nc.vector.tensor_tensor(x[h][:], along[h][:], tce[h][:], ALU.subtract)
+
+        def rescale(h):
+            nc.vector.scalar_tensor_tensor(
+                grouped(wgt[h][:]), grouped(x[h][:]), gains[:], spread(rstd[:, h * HG : (h + 1) * HG]), ALU.mult, ALU.mult
+            )
+
+        multiply(0)
+        sum_ta(0)
+        multiply(1)
+        project(0)
+        sum_ta(1)
+        project(1)
+        slope(0)
+        centre_ta(0)
+        slope(1)
+        centre_ta(1)
+        along_n(0, nc.vector)
+        along_n(1, nc.vector)
         for h in halves:
-            nc.vector.scalar_tensor_tensor(t[h][:], x[h][:], gains[:], wgt[h][:], ALU.mult, ALU.mult)
+            remove_along(h)
+        for h in halves:
+            rescale(h)
+        for h in halves:
+            nc.vector.scalar_tensor_tensor(t[h][:], u2[h][:], -1.0, wgt[h][:], ALU.add, ALU.mult)
         for h in halves:
             cols = slice(h * HJ, (h + 1) * HJ)
             nc.vector.tensor_tensor(y[h][:], t[h][:], base_sb[:, cols], ALU.add)

@@ -134,13 +134,19 @@ def tile_attend_tcgroupscale_kernel(
             nc.vector.scalar_tensor_tensor(
                 grouped(ce[h][:]), spread(a_sum[:, h * HG : (h + 1) * HG]), -1.0 / GROUP, grouped(a[h][:]), ALU.mult, ALU.add
             )
-            nc.scalar.activation(sq[h][:], ce[h][:], ACT.Square)
+        var_late = sb.tile([P, HG], F32, name="var_late")
+        nc.scalar.activation(sq[0][:], ce[0][:], ACT.Square)
+        for g in range(HG):
+            slots = slice(g * GROUP, (g + 1) * GROUP)
+            nc.scalar.activation(
+                sq[1][:, slots], ce[1][:, slots], ACT.Square, accum_out=var_late[:, g : g + 1]
+            )
         ta = [product(dtab_win, dtab_sc, h, "ta") for h in halves]
-        var_sum = sb.tile([P, G], F32, name="var_sum", tag="window_then_var")
-        for h in halves:
-            nc.vector.tensor_reduce(var_sum[:, h * HG : (h + 1) * HG], grouped(sq[h][:]), AXIS_X, ALU.add)
+        var_first = sb.tile([P, HG], F32, name="var_first", tag="window_then_var")
+        nc.vector.tensor_reduce(var_first[:], grouped(sq[0][:]), AXIS_X, ALU.add)
         rstd = sb.tile([P, G], F32, name="rstd")
-        nc.scalar.activation(rstd[:], var_sum[:], ACT.Abs_reciprocal_sqrt, bias=EPS, scale=1.0 / GROUP)
+        nc.scalar.activation(rstd[:, HG:], var_late[:], ACT.Abs_reciprocal_sqrt, bias=EPS, scale=1.0 / GROUP)
+        nc.scalar.activation(rstd[:, :HG], var_first[:], ACT.Abs_reciprocal_sqrt, bias=EPS, scale=1.0 / GROUP)
         rvar = sb.tile([P, G], F32, name="rvar")
         nc.gpsimd.tensor_tensor(rvar[:], rstd[:], rstd[:], ALU.mult)
 
@@ -154,6 +160,7 @@ def tile_attend_tcgroupscale_kernel(
             )
         for h in halves:
             nc.scalar.activation(u[h][:], n[h], ACT.Tanh, bias=bias_c[:], scale=gain_c[:])
+        for h in halves:
             nc.scalar.activation(u2[h][:], u[h][:], ACT.Square)
 
         t_sum, cov, c = narrow("t_sum"), narrow("cov"), narrow("c")

from contextlib import ExitStack

import concourse.mybir as mybir

K, R, T, J, G = 512, 128, 2048, 512, 32
GROUP = J // G
EPS = 0.05
FLOPS = 2 * 2 * K * R * J

F32 = mybir.dt.float32
BF16 = mybir.dt.bfloat16
I32 = mybir.dt.int32
U32 = mybir.dt.uint32
U16 = mybir.dt.uint16
U8 = mybir.dt.uint8
FP8X4 = mybir.dt.float8_e4m3fn_x4
ALU = mybir.AluOpType
ACT = mybir.ActivationFunctionType
AXIS_X = mybir.AxisListType.X

P = 128
PACK = 4
HALVES = 2
HJ = J // HALVES
HG = G // HALVES


def tile_attend_tcgroupscale_kernel(
    tc, tab_words, tab_scales, dtab_words, dtab_scales, w1, gain, bias, og, base, offs, out
):
    nc = tc.nc

    def grouped(ap):
        return ap.rearrange("p (g i) -> p g i", i=GROUP)

    def spread(ap):
        return ap.unsqueeze(2).to_broadcast([P, HG, GROUP])

    with ExitStack() as ctx:
        sb = ctx.enter_context(tc.tile_pool(name="sb", bufs=1))
        ps = ctx.enter_context(tc.psum_pool(name="ps", bufs=1))

        offsets = sb.tile([P, J // 16], U16, name="offsets")
        nc.sync.dma_start(offsets[:], offs)

        tab_plane = sb.tile([P, T], U8, name="tab_plane", align_bytes=64)
        dtab_plane = sb.tile([P, T], U8, name="dtab_plane", tag="plane_then_sum", align_bytes=64)
        nc.vector.memset(tab_plane[:].bitcast(I32), 0)
        nc.vector.memset(dtab_plane[:].bitcast(I32), 0)

        warm_in = sb.tile([P, 1], F32, name="warm_in")
        warm_out = sb.tile([P, 1], F32, name="warm_out")
        nc.gpsimd.memset(warm_in[:], 1.0)

        w_raw = sb.tile([P, PACK, R], F32, name="w_raw")
        nc.sync.dma_start(out=w_raw[:], in_=w1.rearrange("(p t) r -> p t r", t=PACK))

        for q in range(4):
            nc.sync.dma_start(
                out=tab_plane[32 * q : 32 * q + 4, :].bitcast(I32),
                in_=tab_scales[0, 4 * q : 4 * q + 4, :].bitcast(I32),
            )
        tab_win = sb.tile([P, T], U32, name="tab_win")
        nc.sync.dma_start(
            out=tab_win[:].bitcast(I32), in_=tab_words[0].rearrange("p n t -> p (n t)").bitcast(I32)
        )
        for q in range(4):
            nc.sync.dma_start(
                out=dtab_plane[32 * q : 32 * q + 4, :].bitcast(I32),
                in_=dtab_scales[0, 4 * q : 4 * q + 4, :].bitcast(I32),
            )
        dtab_win = sb.tile([P, T], U32, name="dtab_win", tag="window_then_var")
        nc.sync.dma_start(
            out=dtab_win[:].bitcast(I32), in_=dtab_words[0].rearrange("p n t -> p (n t)").bitcast(I32)
        )
        gain_c = sb.tile([P, 1], F32, name="gain_c")
        bias_c = sb.tile([P, 1], F32, name="bias_c")
        og_c = sb.tile([P, 1], F32, name="og_c")
        nc.sync.dma_start(out=gain_c[:], in_=gain)
        nc.sync.dma_start(out=bias_c[:], in_=bias)
        nc.sync.dma_start(out=og_c[:], in_=og)
        base_sb = sb.tile([P, J], F32, name="base_sb")
        nc.sync.dma_start(out=base_sb[:], in_=base)

        gains = sb.tile([P, 1], F32, name="gains")
        nc.gpsimd.tensor_tensor(gains[:], gain_c[:], og_c[:], ALU.mult)

        nc.scalar.activation(warm_out[:], warm_in[:], ACT.Abs_reciprocal_sqrt)

        w_bf = sb.tile([P, R, PACK], BF16, name="w_bf", align_bytes=64)
        nc.vector.tensor_copy(w_bf[:], w_raw[:].rearrange("p t r -> p r t"))
        w_codes = sb.tile([P, R], U32, name="w_codes", align_bytes=64)
        w_scales = sb.tile([P, R], U8, name="w_scales", align_bytes=64)
        nc.vector.quantize_mx(
            out=w_codes[:].bitcast(FP8X4), scales=w_scales[:], in_=w_bf[:].rearrange("p r t -> p (r t)")
        )

        tab_sc = sb.tile([P, J], U8, name="tab_sc", align_bytes=64)
        nc.vector.tensor_copy(tab_sc[:], tab_plane[:].indirect(offsets[:]))

        def product(window, scales, h, name):
            cols = slice(h * HJ, (h + 1) * HJ)
            codes = sb.tile([P, HJ], U32, name=name + "_codes%d" % h, align_bytes=64)
            nc.vector.tensor_copy(codes[:], window[:].indirect(offsets[:, h * HG : (h + 1) * HG]))
            acc = ps.tile([P, HJ], F32, name=name + "_acc%d" % h)
            nc.tensor.matmul_mx(
                out=acc[:],
                lhsT=w_codes[:].bitcast(FP8X4),
                lhsT_scale=w_scales[:],
                rhs=codes[:].bitcast(FP8X4),
                rhs_scale=scales[:, cols],
                start=True,
                stop=True,
            )
            return acc

        def wide(name):
            return [sb.tile([P, HJ], F32, name=name + "%d" % h) for h in range(HALVES)]

        def narrow(name):
            return [sb.tile([P, HG], F32, name=name + "%d" % h) for h in range(HALVES)]

        halves = range(HALVES)
        a = [product(tab_win, tab_sc, h, "a") for h in halves]

        dtab_sc = sb.tile([P, J], U8, name="dtab_sc", align_bytes=64)
        nc.vector.tensor_copy(dtab_sc[:], dtab_plane[:].indirect(offsets[:]))

        ce, sq = wide("ce"), wide("sq")
        a_sum = sb.tile([P, G], F32, name="a_sum", tag="plane_then_sum", align_bytes=64)
        for h in halves:
            nc.vector.tensor_reduce(a_sum[:, h * HG : (h + 1) * HG], grouped(a[h][:]), AXIS_X, ALU.add)
        for h in halves:
            nc.vector.scalar_tensor_tensor(
                grouped(ce[h][:]), spread(a_sum[:, h * HG : (h + 1) * HG]), -1.0 / GROUP, grouped(a[h][:]), ALU.mult, ALU.add
            )
        var_late = sb.tile([P, HG], F32, name="var_late")
        nc.scalar.activation(sq[0][:], ce[0][:], ACT.Square)
        for g in range(HG):
            slots = slice(g * GROUP, (g + 1) * GROUP)
            nc.scalar.activation(
                sq[1][:, slots], ce[1][:, slots], ACT.Square, accum_out=var_late[:, g : g + 1]
            )
        ta = [product(dtab_win, dtab_sc, h, "ta") for h in halves]
        var_first = sb.tile([P, HG], F32, name="var_first", tag="window_then_var")
        nc.vector.tensor_reduce(var_first[:], grouped(sq[0][:]), AXIS_X, ALU.add)
        rstd = sb.tile([P, G], F32, name="rstd")
        nc.scalar.activation(rstd[:, HG:], var_late[:], ACT.Abs_reciprocal_sqrt, bias=EPS, scale=1.0 / GROUP)
        nc.scalar.activation(rstd[:, :HG], var_first[:], ACT.Abs_reciprocal_sqrt, bias=EPS, scale=1.0 / GROUP)
        rvar = sb.tile([P, G], F32, name="rvar")
        nc.gpsimd.tensor_tensor(rvar[:], rstd[:], rstd[:], ALU.mult)


        u, u2 = wide("u"), wide("u2")
        n_all = sb.tile([P, J], F32, name="n_all")
        n = [n_all[:, h * HJ : (h + 1) * HJ] for h in halves]
        for h in halves:
            nc.gpsimd.tensor_tensor(
                grouped(n[h]), grouped(ce[h][:]), spread(rstd[:, h * HG : (h + 1) * HG]), ALU.mult
            )
        for h in halves:
            nc.scalar.activation(u[h][:], n[h], ACT.Tanh, bias=bias_c[:], scale=gain_c[:])
        for h in halves:
            nc.scalar.activation(u2[h][:], u[h][:], ACT.Square)

        t_sum, cov, c = narrow("t_sum"), narrow("cov"), narrow("c")
        tce, prod, along, x, wgt, t, y = (
            wide("tce"), wide("prod"), wide("along"), wide("x"), wide("wgt"), wide("t"), wide("y")
        )

        def sum_ta(h):
            nc.vector.tensor_reduce(t_sum[h][:], grouped(ta[h][:]), AXIS_X, ALU.add)

        def centre_ta(h):
            nc.vector.scalar_tensor_tensor(
                grouped(tce[h][:]), spread(t_sum[h][:]), -1.0 / GROUP, grouped(ta[h][:]), ALU.mult, ALU.add
            )

        def multiply(h):
            nc.vector.scalar_tensor_tensor(prod[h][:], ta[h][:], 1.0 / GROUP, ce[h][:], ALU.mult, ALU.mult)

        def project(h):
            nc.vector.tensor_reduce(cov[h][:], grouped(prod[h][:]), AXIS_X, ALU.add)

        def slope(h):
            nc.vector.tensor_tensor(c[h][:], cov[h][:], rvar[:, h * HG : (h + 1) * HG], ALU.mult)

        def along_n(h, engine):
            engine.tensor_tensor(grouped(along[h][:]), grouped(ce[h][:]), spread(c[h][:]), ALU.mult)

        def remove_along(h):
            nc.vector.tensor_tensor(x[h][:], along[h][:], tce[h][:], ALU.subtract)

        def rescale(h):
            nc.vector.scalar_tensor_tensor(
                grouped(wgt[h][:]), grouped(x[h][:]), gains[:], spread(rstd[:, h * HG : (h + 1) * HG]), ALU.mult, ALU.mult
            )

        multiply(0)
        sum_ta(0)
        multiply(1)
        project(0)
        sum_ta(1)
        project(1)
        slope(0)
        centre_ta(0)
        slope(1)
        centre_ta(1)
        along_n(0, nc.vector)
        along_n(1, nc.vector)
        for h in halves:
            remove_along(h)
        for h in halves:
            rescale(h)
        for h in halves:
            nc.vector.scalar_tensor_tensor(t[h][:], u2[h][:], -1.0, wgt[h][:], ALU.add, ALU.mult)
        for h in halves:
            cols = slice(h * HJ, (h + 1) * HJ)
            nc.vector.tensor_tensor(y[h][:], t[h][:], base_sb[:, cols], ALU.add)
            nc.sync.dma_start(out=out[:, cols], in_=y[h][:])
